import numpy as np
import ml_dtypes


def mxq(x, axis, fmt="e4m3"):
    dtype, down = {"e4m3": (ml_dtypes.float8_e4m3fn, 7), "e5m2": (ml_dtypes.float8_e5m2, 14)}[fmt]
    v = np.moveaxis(np.asarray(x, np.float32).astype(ml_dtypes.bfloat16).astype(np.float64), axis, -1)
    blocks = v.reshape(v.shape[:-1] + (-1, 32))
    amax = np.abs(blocks).max(-1, keepdims=True)
    byte = np.maximum(np.where(amax > 0, np.frexp(amax)[1] - 1 + 127, 0) - down, 1)
    scale = np.exp2(byte - 127.0)
    codes = (blocks / scale).astype(np.float32).astype(dtype).astype(np.float64)
    return np.moveaxis((codes * scale).reshape(v.shape), -1, axis)


WIDE = False


def mx_kscale(k):
    if not WIDE:
        return np.ones(k)
    levels = np.array([10, -10, 5, -5, 0])
    if k % 512:
        return np.exp2(np.random.permutation(np.resize(levels, k // 32))).repeat(32)
    a = np.empty((k // 512, 16))
    for p in range(k // 512):
        a[p, :8] = np.random.permutation(np.resize(levels, 8))
        for g in range(8):
            far = levels[np.abs(levels - a[p, g]) >= 10]
            a[p, g + 8] = far[np.random.randint(len(far))]
    return np.exp2(a.ravel()).repeat(32)


def f64(x):
    return np.asarray(x).astype(np.float64)


def striped(idx):
    return np.tile(idx.reshape(-1, 16).T, (8, 1)).astype(np.uint16)


def unstriped(offs):
    return offs[:16].T.reshape(-1).astype(np.int64)


E2M1 = np.array([0.0, 0.5, 1.0, 1.5, 2.0, 3.0, 4.0, 6.0, -0.0, -0.5, -1.0, -1.5, -2.0, -3.0, -4.0, -6.0])


def pack_weight(w, fmt):
    k, n = w.shape
    w = f64(np.asarray(w, np.float32).astype(ml_dtypes.bfloat16)).reshape(k // 32, 32, n)
    amax = np.abs(w).max(1)
    if fmt == "e4m3":
        byte = np.frexp(amax)[1] - 1 + 127 - 7
    else:
        mant, ex = np.frexp(amax / 6.0)
        byte = np.where(mant > 0.5, ex, ex - 1) + 127
    byte = np.clip(np.where(amax > 0, byte, 1), 1, 254)
    scaled = (w * np.exp2(127.0 - byte)[:, None, :]).reshape(k, n).astype(np.float32)
    by_word = np.ascontiguousarray(scaled.reshape(k // 512, 128, 4, n).transpose(0, 1, 3, 2))
    if fmt == "e4m3":
        words = by_word.astype(ml_dtypes.float8_e4m3fn).view(np.uint8)
    else:
        c = by_word.astype(ml_dtypes.float4_e2m1fn).view(np.uint8) & 0xF
        words = (c[..., 0::2] | (c[..., 1::2] << 4)).reshape(k // 512, 128, 2 * n)
    return np.ascontiguousarray(words), np.ascontiguousarray(byte.astype(np.uint8).reshape(k // 512, 16, n))


def unpack_weight(words, scales, fmt):
    g, _, n = scales.shape
    words = np.ascontiguousarray(words).reshape(g, 128, n, -1)
    if fmt == "e4m3":
        vals = words.view(ml_dtypes.float8_e4m3fn).astype(np.float64)
    else:
        nib = np.empty((g, 128, n, 4), np.uint8)
        nib[..., 0::2] = words & 0xF
        nib[..., 1::2] = words >> 4
        vals = E2M1[nib]
    vals = vals * np.repeat(np.exp2(scales.astype(np.float64) - 127.0), 8, axis=1)[..., None]
    return vals.transpose(0, 1, 3, 2).reshape(g * 512, n)


def gelu(v):
    return 0.5 * v * (1.0 + np.tanh(np.sqrt(2.0 / np.pi) * (v + 0.044715 * v**3)))


T, S, K, H, T2, P = 2048, 512, 1024, 1024, 1024, 512

def setup_inputs():
    n = np.random.standard_normal
    s = mx_kscale(K)[:, None]
    u = mx_kscale(H)[:, None]
    d = {}
    d["tab_words"], d["tab_scales"] = pack_weight(n((K, T)) * s, "e4m3")
    d["offs"] = striped(np.random.permutation(T)[:S])
    d["w1"] = (n((K, H)) / s * u.T / K ** 0.5).astype(np.float32)
    d["w4_words"], d["w4_scales"] = pack_weight(n((K, H)) / s * u.T / K ** 0.5, "e2m1")
    d["prior"] = (n((H, S)) * u).astype(np.float32)
    d["wgs"] = np.exp(0.3 * n((128, S))).astype(np.float32)
    d["page0"] = (n((H, T2)) * u).astype(np.float32)
    d["offs2"] = striped(np.random.permutation(T2)[:S])
    d["offs3"] = striped(np.random.permutation(T2)[:P])
    d["low"] = ((0.6 * n(H) - 0.2) * u[:, 0]).astype(np.float32)
    d["gain"] = (np.random.uniform(-0.65, 0.65, H) / u[:, 0] ** 2 / H ** 0.5).astype(np.float32)
    d["slot"] = np.random.uniform(-1.0, 1.0, T2).astype(np.float32)
    return d

def reference(tab_words, tab_scales, offs, w1, w4_words, w4_scales, prior, wgs, page0, offs2, offs3, low, gain, slot):
    v = unpack_weight(tab_words, tab_scales, "e4m3")[:, unstriped(offs)]
    w4 = unpack_weight(w4_words, w4_scales, "e2m1")
    a = mxq(f64(w1), 0, "e4m3").T @ v
    b = w4.T @ v
    h = np.minimum(np.maximum(a, f64(prior)), b)
    page = f64(page0).copy()
    page[:, unstriped(offs2)] = np.tile(f64(wgs), (H // 128, 1)) * h
    x = page[:, unstriped(offs3)]
    x = np.maximum(x, f64(low)[:, None]) * f64(gain)[:, None]
    e = mxq(page, 0, "e4m3").T @ mxq(x, 0, "e4m3")
    return np.sin(e - f64(slot)[:, None])

@@ -1,0 +1,414 @@
+import math
+from contextlib import ExitStack
+
+import concourse.mybir as mybir
+
+T, S, K, H, T2, NX = 2048, 512, 1024, 1024, 1024, 512
+FLOPS = 2 * (2 * K * H * S + H * T2 * NX)
+
+F32 = mybir.dt.float32
+BF16 = mybir.dt.bfloat16
+I32 = mybir.dt.int32
+U32 = mybir.dt.uint32
+U16 = mybir.dt.uint16
+U8 = mybir.dt.uint8
+FP8X4 = mybir.dt.float8_e4m3fn_x4
+FP4X4 = mybir.dt.float4_e2m1fn_x4
+ALU = mybir.AluOpType
+ACT = mybir.ActivationFunctionType
+
+P = 128
+PACK = 4
+SPAN = P * PACK
+PASSES = 2
+TILES = PASSES * PACK
+CHUNKS = 4
+CW = T2 // CHUNKS
+TWO_PI = 2.0 * math.pi
+VECTOR_ONLY = (0, 4)
+
+
+def tile_list_parcel_boundary_conflicts_kernel(
+    tc, tab_words, tab_scales, offs, w1, w4_words, w4_scales, prior, wgs, page0, offs2, offs3, low, gain, slot, out
+):
+    nc = tc.nc
+    with ExitStack() as ctx:
+        lists = ctx.enter_context(tc.tile_pool(name="lists", bufs=1))
+        keep = ctx.enter_context(tc.tile_pool(name="keep", bufs=1))
+        ring = ctx.enter_context(tc.tile_pool(name="ring", bufs=3))
+        psum = ctx.enter_context(tc.psum_pool(name="psum", bufs=1))
+
+        def held(name, shape, dtype):
+            return keep.tile(shape, dtype, name=name, align_bytes=64)
+
+        idx = lists.tile([P, S // 16], U16, name="idx")
+        idx2 = lists.tile([P, S // 16], U16, name="idx2")
+        idx3 = lists.tile([P, NX // 16], U16, name="idx3")
+
+        tab_w = [held("tab_w%d" % a, [P, T], U32) for a in range(PASSES)]
+        tab_s = held("tab_s", [P, PASSES * T], U8)
+        w4_raw = held("w4_raw", [P, PASSES, 2 * H], U8)
+        w4s_raw = held("w4s_raw", [P, PASSES * H], U8)
+        w1_near = [held("w1_near%d" % i, [P, PASSES, PACK, P], F32) for i in range(PACK)]
+        w1_raw = [held("w1_raw%d" % a, [P, PACK, SPAN], F32) for a in range(PASSES)]
+        prior_sb = [held("prior%d" % i, [P, S], F32) for i in range(TILES)]
+        page = [held("page%d" % i, [P, T2], F32) for i in range(TILES)]
+        wgs_near = held("wgs_near", [P, S], F32)
+        wgs_dealt = held("wgs_dealt", [P, PACK, S], F32)
+        low_sb = [held("low%d" % b, [P, PACK], F32) for b in range(PASSES)]
+        gain_sb = [held("gain%d" % b, [P, PACK], F32) for b in range(PASSES)]
+        slot_sb = held("slot_sb", [P, T2 // P], F32)
+        neg_slot = held("neg_slot", [P, T2 // P], F32)
+        warm_in = held("warm_in", [P, 1], F32)
+        warm_out = held("warm_out", [P, 1], F32)
+
+        nc.vector.memset(tab_s[:].bitcast(I32), 0)
+        nc.vector.memset(w4s_raw[:].bitcast(I32), 0)
+        nc.vector.memset(warm_in[:], 0.0)
+        nc.scalar.activation(warm_out[:], warm_in[:], ACT.Sin)
+
+        def load_tab(a):
+            nc.sync.dma_start(tab_w[a][:].bitcast(I32), tab_words[a].rearrange("p t i -> p (t i)").bitcast(I32))
+
+        def load_planes(dst, src):
+            rows = src.bitcast(I32).rearrange("a (q r) n -> r q a n", r=4)
+            for r in range(4):
+                nc.sync.dma_start(dst[r:P:32, :].bitcast(I32).rearrange("p (a n) -> p a n", a=PASSES), rows[r])
+
+        def load_w1_near(i):
+            for a in range(PASSES):
+                rows = w1[a * SPAN : (a + 1) * SPAN, i * P : (i + 1) * P]
+                nc.sync.dma_start(w1_near[i][:, a], rows.rearrange("(p j) c -> p j c", j=PACK))
+
+        def load_w1(a):
+            rows = w1[a * SPAN : (a + 1) * SPAN, SPAN : 2 * SPAN]
+            nc.sync.dma_start(w1_raw[a][:], rows.rearrange("(p j) c -> p j c", j=PACK))
+
+        def rows_of(src, i):
+            if i < PACK:
+                return src[i * P : (i + 1) * P, :]
+            return src[SPAN:, :].rearrange("(p t) n -> t p n", t=PACK)[i - PACK]
+
+        def load_prior(i):
+            nc.sync.dma_start(prior_sb[i][:], rows_of(prior, i))
+
+        def load_page(i):
+            nc.sync.dma_start(page[i][:], rows_of(page0, i))
+
+        nc.sync.dma_start(idx[:], offs)
+        load_tab(0)
+        load_planes(tab_s, tab_scales)
+        load_tab(1)
+        load_w1_near(0)
+        nc.sync.dma_start(w4_raw[:].bitcast(I32), w4_words.bitcast(I32).rearrange("a p n -> p a n"))
+        load_planes(w4s_raw, w4_scales)
+        load_prior(0)
+        nc.sync.dma_start(wgs_near[:], wgs)
+        nc.sync.dma_start(idx2[:], offs2)
+        load_w1_near(1)
+        load_page(0)
+        load_prior(1)
+        nc.sync.dma_start(idx3[:], offs3)
+        with nc.allow_non_contiguous_dma(reason="one value for each partition"):
+            nc.sync.dma_start(low_sb[0][:], low[:SPAN].rearrange("(c p) -> p c", p=P))
+            nc.sync.dma_start(gain_sb[0][:], gain[:SPAN].rearrange("(c p) -> p c", p=P))
+        load_w1_near(2)
+        load_page(1)
+        load_prior(2)
+        load_w1_near(3)
+        load_page(2)
+        load_prior(3)
+        load_w1(0)
+        load_w1(1)
+        load_page(3)
+        load_prior(4)
+
+        def load_late(i):
+            if i == 0:
+                for q in (0, 2, 1, 3):
+                    nc.sync.dma_start(wgs_dealt[32 * q : 32 * q + 32], wgs.rearrange("(q t) j -> q t j", t=PACK))
+                nc.sync.dma_start(low_sb[1][:], low[SPAN:].rearrange("(p t) -> p t", t=PACK))
+                nc.sync.dma_start(gain_sb[1][:], gain[SPAN:].rearrange("(p t) -> p t", t=PACK))
+            load_page(PACK + i)
+            if PACK + i + 1 < TILES:
+                load_prior(PACK + i + 1)
+            else:
+                with nc.allow_non_contiguous_dma(reason="one value for each partition"):
+                    nc.sync.dma_start(slot_sb[:], slot.rearrange("(c p) -> p c", p=P))
+
+        v_w = [held("v_w%d" % a, [P, S], U32) for a in range(PASSES)]
+        v_s = [held("v_s%d" % a, [P, S], U8) for a in range(PASSES)]
+
+        def pick_words(a):
+            nc.vector.tensor_copy(v_w[a][:], tab_w[a][:].indirect(idx[:]))
+
+        def pick_scales(a):
+            nc.vector.tensor_copy(v_s[a][:], tab_s[:, a * T : (a + 1) * T].indirect(idx[:]))
+
+        w4_c = [held("w4_c%d" % a, [P, PACK, 2 * P], U8) for a in range(PASSES)]
+        w4_s = [held("w4_s%d" % a, [P, PACK, P], U8) for a in range(PASSES)]
+        w1_b = {}
+        w1_c = {}
+        w1_s = {}
+
+        def deal_w4(a):
+            src = w4_raw[:, a, 2 * SPAN :].bitcast(U16).rearrange("p (q t) -> p t q", t=PACK)
+            nc.vector.tensor_copy(w4_c[a][:].bitcast(U16), src)
+
+        def deal_w4_scales(a):
+            src = w4s_raw[:, a * H + SPAN : (a + 1) * H].rearrange("p (q t) -> p t q", t=PACK)
+            nc.vector.tensor_copy(w4_s[a][:], src)
+
+        def round_w1_near(i):
+            w1_b[i] = ring.tile([P, 2, P, PACK], BF16, name="w1_b", align_bytes=64, bufs=4)
+            for a in range(PASSES):
+                nc.scalar.copy(
+                    w1_b[i][:, a].rearrange("p (c e) j -> p c j e", e=4),
+                    w1_near[i][:, a].rearrange("p j (c e) -> p c j e", e=4),
+                )
+
+        def round_w1(a, u):
+            w1_b[a, u] = ring.tile([P, 2, P, PACK], BF16, name="w1_b", align_bytes=64, bufs=4)
+            nc.scalar.copy(
+                w1_b[a, u][:].rearrange("p t q j -> p q j t"),
+                w1_raw[a][:].rearrange("p j (q t) -> p q j t", t=PACK)[:, :, :, 2 * u : 2 * u + 2],
+            )
+
+        def quantize_w1(key):
+            name = "%d" % key if isinstance(key, int) else "%d%d" % key
+            w1_c[key] = held("w1_c" + name, [P, 2 * P], U32)
+            w1_s[key] = held("w1_s" + name, [P, 2 * P], U8)
+            nc.vector.quantize_mx(w1_c[key][:].bitcast(FP8X4), w1_s[key][:], w1_b[key][:].rearrange("p t q j -> p (t q j)"))
+
+        def bank(n):
+            return psum.tile([P, 512], F32, name="bank%d" % (n % 8))
+
+        sums = {}
+
+        def first_products(i):
+            first = bank(2 * i)
+            second = bank(2 * i + 1)
+            for a in range(PASSES):
+                if i < PACK:
+                    key, e = i, a
+                else:
+                    key, e = (a, (i - PACK) // 2), i % 2
+                cols = slice(e * P, (e + 1) * P)
+                nc.tensor.matmul_mx(
+                    first[:], w1_c[key][:, cols].bitcast(FP8X4), w1_s[key][:, cols],
+                    v_w[a][:].bitcast(FP8X4), v_s[a][:], start=(a == 0), stop=(a == PASSES - 1),
+                )
+            for a in range(PASSES):
+                if i < PACK:
+                    codes = w4_raw[:, a, 2 * P * i : 2 * P * (i + 1)]
+                    scales = w4s_raw[:, a * H + P * i : a * H + P * (i + 1)]
+                else:
+                    codes = w4_c[a][:, i - PACK, :]
+                    scales = w4_s[a][:, i - PACK, :]
+                nc.tensor.matmul_mx(
+                    second[:], codes.bitcast(FP4X4), scales,
+                    v_w[a][:].bitcast(FP8X4), v_s[a][:], start=(a == 0), stop=(a == PASSES - 1),
+                )
+            sums[i] = (first, second)
+
+        raised = {}
+        h = {}
+        picked = {}
+
+        def raise_to_prior(i):
+            raised[i] = ring.tile([P, S], F32, name="work_a")
+            nc.vector.tensor_tensor(raised[i][:], sums[i][0][:], prior_sb[i][:], ALU.max)
+
+        def cap(i):
+            if i == TILES - 1:
+                h[i] = held("x_b0", [P, S], F32)
+            else:
+                h[i] = ring.tile([P, S], F32, name="work_b")
+            nc.vector.tensor_tensor(h[i][:], sums[i][1][:], raised[i][:], ALU.min)
+
+        def put(i):
+            factors = wgs_near[:] if i < PACK else wgs_dealt[:, i - PACK, :]
+            nc.vector.tensor_tensor(page[i][:].indirect(idx2[:]), h[i][:], factors, ALU.mult)
+
+        def fetch(i):
+            picked[i] = ring.tile([P, NX], F32, name="work_c")
+            nc.vector.tensor_copy(picked[i][:], page[i][:].indirect(idx3[:]))
+
+        page_b = {(b, c): held("page_b%d%d" % (b, c), [P, CW, PACK], BF16) for b in range(PASSES) for c in range(CHUNKS)}
+        page_c = {(b, c): held("page_c%d%d" % (b, c), [P, CW], U32) for b in range(PASSES) for c in range(CHUNKS)}
+        page_s = {(b, c): held("page_s%d%d" % (b, c), [P, CW], U8) for b in range(PASSES) for c in range(CHUNKS)}
+        x_b = [held("x_b0", [P, NX, PACK], BF16)]
+        x_c = [held("x_c%d" % b, [P, NX], U32) for b in range(PASSES)]
+        x_s = [held("x_s%d" % b, [P, NX], U8) for b in range(PASSES)]
+        x_pair = held("x_pair", [P, 2, NX], BF16)
+        gathered = held("gathered", [P, PACK, T2 + NX], BF16)
+        near = {}
+
+        staged = []
+
+        def round_page(i):
+            if i < PACK:
+                near[i] = held("near%d" % i, [P, T2 + NX], BF16)
+                nc.scalar.copy(near[i][:, :T2], page[i][:])
+            elif i < TILES - 1:
+                nc.scalar.copy(staged[0][:, i - PACK, :], page[i][:])
+                if i == TILES - 2:
+                    for c in range(CHUNKS):
+                        nc.scalar.copy(
+                            page_b[1, c][:, :, : PACK - 1],
+                            staged[0][:, :, c * CW : (c + 1) * CW].rearrange("p t m -> p m t"),
+                        )
+            else:
+                for c in range(CHUNKS):
+                    nc.scalar.copy(page_b[1, c][:, :, PACK - 1], page[i][:, c * CW : (c + 1) * CW])
+
+        def move_rows(i):
+            for t in range(PACK):
+                nc.sync.dma_start(gathered[32 * i : 32 * (i + 1), t, :], near[i][t:P:PACK, :])
+
+        def weave():
+            for c in range(CHUNKS):
+                nc.scalar.copy(
+                    page_b[0, c][:].rearrange("p (m e) t -> p m t e", e=4),
+                    gathered[:, :, c * CW : (c + 1) * CW].rearrange("p t (m e) -> p m t e", e=4),
+                )
+            nc.scalar.copy(
+                x_b[0][:].rearrange("p (m e) t -> p m t e", e=4),
+                gathered[:, :, T2:].rearrange("p t (m e) -> p m t e", e=4),
+            )
+
+        def quantize_page(b, c):
+            nc.vector.quantize_mx(page_c[b, c][:].bitcast(FP8X4), page_s[b, c][:], page_b[b, c][:].rearrange("p m t -> p (m t)"))
+
+        def make_x(i):
+            b, t = divmod(i, PACK)
+            if b == 0:
+                dst = near[i][:, T2:]
+            elif t < 2:
+                dst = x_pair[:, t, :]
+            else:
+                dst = x_b[b][:, :, t]
+            nc.vector.tensor_scalar(dst, picked[i][:], low_sb[b][:, t : t + 1], gain_sb[b][:, t : t + 1], ALU.max, ALU.mult)
+            if b == 0:
+                move_rows(i)
+                load_late(i)
+            elif t == 1:
+                nc.scalar.copy(x_b[b][:, :, 0:2], x_pair[:].rearrange("p e j -> p j e"))
+
+        def quantize_x(b):
+            nc.vector.quantize_mx(x_c[b][:].bitcast(FP8X4), x_s[b][:], x_b[b][:].rearrange("p j t -> p (j t)"))
+
+        scores = {}
+
+        def last_product(n, b):
+            c, half = divmod(n, CW // P)
+            cols = slice(half * P, (half + 1) * P)
+            if b == 0:
+                scores[n] = bank(n)
+            nc.tensor.matmul_mx(
+                scores[n][:], page_c[b, c][:, cols].bitcast(FP8X4), page_s[b, c][:, cols],
+                x_c[b][:].bitcast(FP8X4), x_s[b][:], start=(b == 0), stop=(b == PASSES - 1),
+            )
+
+        pick_words(0)
+        pick_scales(0)
+        pick_scales(1)
+        pick_words(1)
+        round_w1_near(0)
+        quantize_w1(0)
+        first_products(0)
+        for a in range(PASSES):
+            deal_w4(a)
+        raise_to_prior(0)
+        deal_w4_scales(0)
+        cap(0)
+        deal_w4_scales(1)
+        round_w1_near(1)
+        quantize_w1(1)
+        first_products(1)
+
+        for i in range(TILES - 1):
+            put(i)
+            if i + 2 < PACK:
+                round_w1_near(i + 2)
+            if i == 1:
+                round_w1(0, 0)
+                round_w1(1, 0)
+            if i == 2:
+                round_w1(0, 1)
+                round_w1(1, 1)
+            round_page(i)
+            raise_to_prior(i + 1)
+            fetch(i)
+            if i == TILES - 2:
+                for c in range(CHUNKS):
+                    quantize_page(0, c)
+                quantize_x(0)
+            cap(i + 1)
+            make_x(i)
+            if i + 2 < PACK:
+                quantize_w1(i + 2)
+            if i == 2:
+                quantize_w1((0, 0))
+                quantize_w1((1, 0))
+            if i == 3:
+                quantize_w1((0, 1))
+                quantize_w1((1, 1))
+            if i + 2 < TILES:
+                first_products(i + 2)
+            if i == 3:
+                weave()
+                staged.append(held("gathered", [P, PACK - 1, T2], BF16))
+                x_b.append(held("near3", [P, NX, PACK], BF16))
+        for n in range(TILES):
+            last_product(n, 0)
+        last = TILES - 1
+        nc.vector.tensor_scalar(neg_slot[:], slot_sb[:], -1.0, None, ALU.mult)
+        put(last)
+        round_page(last)
+        fetch(last)
+        quantize_page(1, 0)
+        make_x(last)
+        quantize_x(1)
+        quantize_page(1, 1)
+        quantize_page(1, 2)
+        quantize_page(1, 3)
+        for n in range(TILES):
+            last_product(n, 1)
+
+        shifted = {}
+        turns = {}
+        reduced = {}
+
+        def shift(n):
+            if n not in VECTOR_ONLY:
+                shifted[n] = ring.tile([P, NX], F32, name="shifted", bufs=4)
+                nc.scalar.activation(shifted[n][:], scores[n][:], ACT.Identity, bias=neg_slot[:, n : n + 1])
+
+        def count_turns(n):
+            turns[n] = ring.tile([P, NX], I32, name="work_a")
+            if n in VECTOR_ONLY:
+                nc.vector.tensor_scalar(turns[n][:], scores[n][:], slot_sb[:, n : n + 1], 1.0 / TWO_PI, ALU.subtract, ALU.mult)
+            else:
+                nc.vector.tensor_scalar(turns[n][:], shifted[n][:], 1.0 / TWO_PI, None, ALU.mult)
+
+        def finish(n):
+            reduced[n] = ring.tile([P, NX], F32, name="work_b")
+            result = held("prior%d" % n, [P, NX], F32)
+            if n in VECTOR_ONLY:
+                nc.vector.scalar_tensor_tensor(reduced[n][:], turns[n][:], -TWO_PI, scores[n][:], ALU.mult, ALU.add)
+                nc.scalar.activation(result[:], reduced[n][:], ACT.Sin, bias=neg_slot[:, n : n + 1])
+            else:
+                nc.vector.scalar_tensor_tensor(reduced[n][:], turns[n][:], -TWO_PI, shifted[n][:], ALU.mult, ALU.add)
+                nc.scalar.activation(result[:], reduced[n][:], ACT.Sin)
+            nc.sync.dma_start(out[n * P : (n + 1) * P, :], result[:])
+
+        shift(1)
+        shift(2)
+        count_turns(0)
+        for n in range(TILES):
+            if n + 3 < TILES:
+                shift(n + 3)
+            if n + 1 < TILES:
+                count_turns(n + 1)
+            finish(n)

@@ -22,8 +22,8 @@ PACK = 4
 SPAN = P * PACK
 PASSES = 2
 TILES = PASSES * PACK
-CHUNKS = 4
-CW = T2 // CHUNKS
+CHUNK_EDGES = (0, 128, 256, 512, 1024)
+CHUNKS = len(CHUNK_EDGES) - 1
 TWO_PI = 2.0 * math.pi
 VECTOR_ONLY = (0, 4)
 
@@ -97,16 +97,16 @@ def tile_list_parcel_boundary_conflicts_kernel(
 
         nc.sync.dma_start(idx[:], offs)
         load_tab(0)
+        load_w1_near(0)
         load_planes(tab_s, tab_scales)
         load_tab(1)
-        load_w1_near(0)
         nc.sync.dma_start(w4_raw[:].bitcast(I32), w4_words.bitcast(I32).rearrange("a p n -> p a n"))
         load_planes(w4s_raw, w4_scales)
         load_prior(0)
         nc.sync.dma_start(wgs_near[:], wgs)
+        load_page(0)
         nc.sync.dma_start(idx2[:], offs2)
         load_w1_near(1)
-        load_page(0)
         load_prior(1)
         nc.sync.dma_start(idx3[:], offs3)
         with nc.allow_non_contiguous_dma(reason="one value for each partition"):
@@ -160,7 +160,7 @@ def tile_list_parcel_boundary_conflicts_kernel(
             nc.vector.tensor_copy(w4_s[a][:], src)
 
         def round_w1_near(i):
-            w1_b[i] = ring.tile([P, 2, P, PACK], BF16, name="w1_b", align_bytes=64, bufs=4)
+            w1_b[i] = ring.tile([P, 2, P, PACK], BF16, name="w1_b", align_bytes=64, bufs=6)
             for a in range(PASSES):
                 nc.scalar.copy(
                     w1_b[i][:, a].rearrange("p (c e) j -> p c j e", e=4),
@@ -168,7 +168,7 @@ def tile_list_parcel_boundary_conflicts_kernel(
                 )
 
         def round_w1(a, u):
-            w1_b[a, u] = ring.tile([P, 2, P, PACK], BF16, name="w1_b", align_bytes=64, bufs=4)
+            w1_b[a, u] = ring.tile([P, 2, P, PACK], BF16, name="w1_b", align_bytes=64, bufs=6)
             nc.scalar.copy(
                 w1_b[a, u][:].rearrange("p t q j -> p q j t"),
                 w1_raw[a][:].rearrange("p j (q t) -> p q j t", t=PACK)[:, :, :, 2 * u : 2 * u + 2],
@@ -221,7 +221,7 @@ def tile_list_parcel_boundary_conflicts_kernel(
 
         def cap(i):
             if i == TILES - 1:
-                h[i] = held("x_b0", [P, S], F32)
+                h[i] = held("page%d" % (i - 1), [P, S], F32)
             else:
                 h[i] = ring.tile([P, S], F32, name="work_b")
             nc.vector.tensor_tensor(h[i][:], sums[i][1][:], raised[i][:], ALU.min)
@@ -231,16 +231,27 @@ def tile_list_parcel_boundary_conflicts_kernel(
             nc.vector.tensor_tensor(page[i][:].indirect(idx2[:]), h[i][:], factors, ALU.mult)
 
         def fetch(i):
-            picked[i] = ring.tile([P, NX], F32, name="work_c")
+            if i == TILES - 1:
+                picked[i] = held("gathered", [P, NX], F32)
+            elif i == TILES - 2:
+                picked[i] = held("x_b0", [P, NX], F32)
+            else:
+                picked[i] = ring.tile([P, NX], F32, name="work_c")
             nc.vector.tensor_copy(picked[i][:], page[i][:].indirect(idx3[:]))
 
-        page_b = {(b, c): held("page_b%d%d" % (b, c), [P, CW, PACK], BF16) for b in range(PASSES) for c in range(CHUNKS)}
-        page_c = {(b, c): held("page_c%d%d" % (b, c), [P, CW], U32) for b in range(PASSES) for c in range(CHUNKS)}
-        page_s = {(b, c): held("page_s%d%d" % (b, c), [P, CW], U8) for b in range(PASSES) for c in range(CHUNKS)}
+        def width(c):
+            return CHUNK_EDGES[c + 1] - CHUNK_EDGES[c]
+
+        def span(c):
+            return slice(CHUNK_EDGES[c], CHUNK_EDGES[c + 1])
+
+        page_b = {(b, c): held("page_b%d%d" % (b, c), [P, width(c), PACK], BF16) for b in range(PASSES) for c in range(CHUNKS)}
+        page_c = {}
+        page_s = {(b, c): held("page_s%d%d" % (b, c), [P, width(c)], U8) for b in range(PASSES) for c in range(CHUNKS)}
         x_b = [held("x_b0", [P, NX, PACK], BF16)]
         x_c = [held("x_c%d" % b, [P, NX], U32) for b in range(PASSES)]
         x_s = [held("x_s%d" % b, [P, NX], U8) for b in range(PASSES)]
-        x_pair = held("x_pair", [P, 2, NX], BF16)
+        x_pair = [held("x_pair%d" % u, [P, 2, NX], BF16) for u in range(2)]
         gathered = held("gathered", [P, PACK, T2 + NX], BF16)
         near = {}
 
@@ -248,7 +259,7 @@ def tile_list_parcel_boundary_conflicts_kernel(
 
         def round_page(i):
             if i < PACK:
-                near[i] = held("near%d" % i, [P, T2 + NX], BF16)
+                near[i] = held(("w1_near1", "w1_near2", "w1_raw0", "w1_raw1")[i], [P, T2 + NX], BF16)
                 nc.scalar.copy(near[i][:, :T2], page[i][:])
             elif i < TILES - 1:
                 nc.scalar.copy(staged[0][:, i - PACK, :], page[i][:])
@@ -256,11 +267,11 @@ def tile_list_parcel_boundary_conflicts_kernel(
                     for c in range(CHUNKS):
                         nc.scalar.copy(
                             page_b[1, c][:, :, : PACK - 1],
-                            staged[0][:, :, c * CW : (c + 1) * CW].rearrange("p t m -> p m t"),
+                            staged[0][:, :, span(c)].rearrange("p t m -> p m t"),
                         )
             else:
                 for c in range(CHUNKS):
-                    nc.scalar.copy(page_b[1, c][:, :, PACK - 1], page[i][:, c * CW : (c + 1) * CW])
+                    nc.scalar.copy(page_b[1, c][:, :, PACK - 1], page[i][:, span(c)])
 
         def move_rows(i):
             for t in range(PACK):
@@ -270,7 +281,7 @@ def tile_list_parcel_boundary_conflicts_kernel(
             for c in range(CHUNKS):
                 nc.scalar.copy(
                     page_b[0, c][:].rearrange("p (m e) t -> p m t e", e=4),
-                    gathered[:, :, c * CW : (c + 1) * CW].rearrange("p t (m e) -> p m t e", e=4),
+                    gathered[:, :, span(c)].rearrange("p t (m e) -> p m t e", e=4),
                 )
             nc.scalar.copy(
                 x_b[0][:].rearrange("p (m e) t -> p m t e", e=4),
@@ -278,22 +289,25 @@ def tile_list_parcel_boundary_conflicts_kernel(
             )
 
         def quantize_page(b, c):
+            name = "x_pair1" if (b, c) == (1, CHUNKS - 1) else "page_c%d%d" % (b, c)
+            page_c[b, c] = held(name, [P, width(c)], U32)
             nc.vector.quantize_mx(page_c[b, c][:].bitcast(FP8X4), page_s[b, c][:], page_b[b, c][:].rearrange("p m t -> p (m t)"))
 
         def make_x(i):
             b, t = divmod(i, PACK)
             if b == 0:
                 dst = near[i][:, T2:]
-            elif t < 2:
-                dst = x_pair[:, t, :]
             else:
-                dst = x_b[b][:, :, t]
+                dst = x_pair[t // 2][:, t % 2, :]
             nc.vector.tensor_scalar(dst, picked[i][:], low_sb[b][:, t : t + 1], gain_sb[b][:, t : t + 1], ALU.max, ALU.mult)
             if b == 0:
                 move_rows(i)
                 load_late(i)
             elif t == 1:
-                nc.scalar.copy(x_b[b][:, :, 0:2], x_pair[:].rearrange("p e j -> p j e"))
+                nc.scalar.copy(x_b[b][:, :, 0:2], x_pair[0][:].rearrange("p e j -> p j e"))
+
+        def weave_last_pair():
+            nc.vector.tensor_copy(x_b[1][:, :, 2:4], x_pair[1][:].rearrange("p e j -> p j e"))
 
         def quantize_x(b):
             nc.vector.quantize_mx(x_c[b][:].bitcast(FP8X4), x_s[b][:], x_b[b][:].rearrange("p j t -> p (j t)"))
@@ -301,8 +315,8 @@ def tile_list_parcel_boundary_conflicts_kernel(
         scores = {}
 
         def last_product(n, b):
-            c, half = divmod(n, CW // P)
-            cols = slice(half * P, (half + 1) * P)
+            c = max(k for k in range(CHUNKS) if CHUNK_EDGES[k] <= n * P)
+            cols = slice(n * P - CHUNK_EDGES[c], (n + 1) * P - CHUNK_EDGES[c])
             if b == 0:
                 scores[n] = bank(n)
             nc.tensor.matmul_mx(
@@ -311,11 +325,11 @@ def tile_list_parcel_boundary_conflicts_kernel(
             )
 
         pick_words(0)
+        round_w1_near(0)
         pick_scales(0)
+        quantize_w1(0)
         pick_scales(1)
         pick_words(1)
-        round_w1_near(0)
-        quantize_w1(0)
         first_products(0)
         for a in range(PASSES):
             deal_w4(a)
@@ -334,16 +348,15 @@ def tile_list_parcel_boundary_conflicts_kernel(
             if i == 1:
                 round_w1(0, 0)
                 round_w1(1, 0)
-            if i == 2:
                 round_w1(0, 1)
                 round_w1(1, 1)
             round_page(i)
             raise_to_prior(i + 1)
-            fetch(i)
             if i == TILES - 2:
                 for c in range(CHUNKS):
                     quantize_page(0, c)
                 quantize_x(0)
+            fetch(i)
             cap(i + 1)
             make_x(i)
             if i + 2 < PACK:
@@ -359,26 +372,26 @@ def tile_list_parcel_boundary_conflicts_kernel(
             if i == 3:
                 weave()
                 staged.append(held("gathered", [P, PACK - 1, T2], BF16))
-                x_b.append(held("near3", [P, NX, PACK], BF16))
+                x_b.append(held("w1_raw1", [P, NX, PACK], BF16))
         for n in range(TILES):
             last_product(n, 0)
         last = TILES - 1
-        nc.vector.tensor_scalar(neg_slot[:], slot_sb[:], -1.0, None, ALU.mult)
+        nc.scalar.activation(neg_slot[:], slot_sb[:], ACT.Copy, scale=-1.0)
         put(last)
         round_page(last)
         fetch(last)
         quantize_page(1, 0)
         make_x(last)
-        quantize_x(1)
         quantize_page(1, 1)
+        weave_last_pair()
         quantize_page(1, 2)
+        quantize_x(1)
         quantize_page(1, 3)
         for n in range(TILES):
             last_product(n, 1)
 
         shifted = {}
         turns = {}
-        reduced = {}
 
         def shift(n):
             if n not in VECTOR_ONLY:
@@ -386,22 +399,29 @@ def tile_list_parcel_boundary_conflicts_kernel(
                 nc.scalar.activation(shifted[n][:], scores[n][:], ACT.Identity, bias=neg_slot[:, n : n + 1])
 
         def count_turns(n):
-            turns[n] = ring.tile([P, NX], I32, name="work_a")
+            if n == 0:
+                turns[n] = held("page_b1%d" % (CHUNKS - 1), [P, NX], I32)
+            else:
+                turns[n] = ring.tile([P, NX], I32, name="work_a")
             if n in VECTOR_ONLY:
                 nc.vector.tensor_scalar(turns[n][:], scores[n][:], slot_sb[:, n : n + 1], 1.0 / TWO_PI, ALU.subtract, ALU.mult)
             else:
                 nc.vector.tensor_scalar(turns[n][:], shifted[n][:], 1.0 / TWO_PI, None, ALU.mult)
 
         def finish(n):
-            reduced[n] = ring.tile([P, NX], F32, name="work_b")
-            result = held("prior%d" % n, [P, NX], F32)
-            if n in VECTOR_ONLY:
-                nc.vector.scalar_tensor_tensor(reduced[n][:], turns[n][:], -TWO_PI, scores[n][:], ALU.mult, ALU.add)
-                nc.scalar.activation(result[:], reduced[n][:], ACT.Sin, bias=neg_slot[:, n : n + 1])
-            else:
-                nc.vector.scalar_tensor_tensor(reduced[n][:], turns[n][:], -TWO_PI, shifted[n][:], ALU.mult, ALU.add)
-                nc.scalar.activation(result[:], reduced[n][:], ACT.Sin)
-            nc.sync.dma_start(out[n * P : (n + 1) * P, :], result[:])
+            parts = 2 if n == TILES - 1 else 1
+            wide = NX // parts
+            for part in range(parts):
+                cols = slice(part * wide, (part + 1) * wide)
+                reduced = ring.tile([P, wide], F32, name="work_b")
+                result = held("result%d" % part if parts > 1 else "prior%d" % n, [P, wide], F32)
+                if n in VECTOR_ONLY:
+                    nc.vector.scalar_tensor_tensor(reduced[:], turns[n][:, cols], -TWO_PI, scores[n][:, cols], ALU.mult, ALU.add)
+                    nc.scalar.activation(result[:], reduced[:], ACT.Sin, bias=neg_slot[:, n : n + 1])
+                else:
+                    nc.vector.scalar_tensor_tensor(reduced[:], turns[n][:, cols], -TWO_PI, shifted[n][:, cols], ALU.mult, ALU.add)
+                    nc.scalar.activation(result[:], reduced[:], ACT.Sin)
+                nc.sync.dma_start(out[n * P : (n + 1) * P, cols], result[:])
 
         shift(1)
         shift(2)

@@ -2,6 +2,7 @@ import math
 from contextlib import ExitStack
 
 import concourse.mybir as mybir
+from concourse.masks import make_identity
 
 T, S, K, H, T2, NX = 2048, 512, 1024, 1024, 1024, 512
 FLOPS = 2 * (2 * K * H * S + H * T2 * NX)
@@ -24,6 +25,7 @@ PASSES = 2
 TILES = PASSES * PACK
 CHUNK_EDGES = (0, 128, 256, 512, 1024)
 CHUNKS = len(CHUNK_EDGES) - 1
+VEC_ROWS = 6
 TWO_PI = 2.0 * math.pi
 VECTOR_ONLY = (0, 4)
 
@@ -55,16 +57,19 @@ def tile_list_parcel_boundary_conflicts_kernel(
         page = [held("page%d" % i, [P, T2], F32) for i in range(TILES)]
         wgs_near = held("wgs_near", [P, S], F32)
         wgs_dealt = held("wgs_dealt", [P, PACK, S], F32)
-        low_sb = [held("low%d" % b, [P, PACK], F32) for b in range(PASSES)]
-        gain_sb = [held("gain%d" % b, [P, PACK], F32) for b in range(PASSES)]
-        slot_sb = held("slot_sb", [P, T2 // P], F32)
-        neg_slot = held("neg_slot", [P, T2 // P], F32)
+        vec_rows = held("vec_rows", [P, SPAN], F32)
+        ident = held("ident", [P, P], F32)
+        near_cols = held("near_cols", [P, PACK, VEC_ROWS], F32)
+        dealt_cols = held("dealt_cols", [P, PACK, 2], F32)
+        neg_slot = held("neg_slot", [P, PACK, 2], F32)
         warm_in = held("warm_in", [P, 1], F32)
         warm_out = held("warm_out", [P, 1], F32)
 
         nc.vector.memset(tab_s[:].bitcast(I32), 0)
         nc.vector.memset(w4s_raw[:].bitcast(I32), 0)
         nc.vector.memset(warm_in[:], 0.0)
+        nc.gpsimd.memset(vec_rows[:], 0.0)
+        make_identity(nc, ident[:])
         nc.scalar.activation(warm_out[:], warm_in[:], ACT.Sin)
 
         def load_tab(a):
@@ -109,9 +114,9 @@ def tile_list_parcel_boundary_conflicts_kernel(
         load_w1_near(1)
         load_prior(1)
         nc.sync.dma_start(idx3[:], offs3)
-        with nc.allow_non_contiguous_dma(reason="one value for each partition"):
-            nc.sync.dma_start(low_sb[0][:], low[:SPAN].rearrange("(c p) -> p c", p=P))
-            nc.sync.dma_start(gain_sb[0][:], gain[:SPAN].rearrange("(c p) -> p c", p=P))
+        nc.sync.dma_start(vec_rows[0:3:2, :], low.rearrange("(b n) -> b n", b=PASSES))
+        nc.sync.dma_start(vec_rows[1:4:2, :], gain.rearrange("(b n) -> b n", b=PASSES))
+        nc.sync.dma_start(vec_rows[4:6, :], slot.rearrange("(b n) -> b n", b=2))
         load_w1_near(2)
         load_page(1)
         load_prior(2)
@@ -127,14 +132,9 @@ def tile_list_parcel_boundary_conflicts_kernel(
             if i == 0:
                 for q in (0, 2, 1, 3):
                     nc.sync.dma_start(wgs_dealt[32 * q : 32 * q + 32], wgs.rearrange("(q t) j -> q t j", t=PACK))
-                nc.sync.dma_start(low_sb[1][:], low[SPAN:].rearrange("(p t) -> p t", t=PACK))
-                nc.sync.dma_start(gain_sb[1][:], gain[SPAN:].rearrange("(p t) -> p t", t=PACK))
             load_page(PACK + i)
             if PACK + i + 1 < TILES:
                 load_prior(PACK + i + 1)
-            else:
-                with nc.allow_non_contiguous_dma(reason="one value for each partition"):
-                    nc.sync.dma_start(slot_sb[:], slot.rearrange("(c p) -> p c", p=P))
 
         v_w = [held("v_w%d" % a, [P, S], U32) for a in range(PASSES)]
         v_s = [held("v_s%d" % a, [P, S], U8) for a in range(PASSES)]
@@ -182,6 +182,18 @@ def tile_list_parcel_boundary_conflicts_kernel(
 
         def bank(n):
             return psum.tile([P, 512], F32, name="bank%d" % (n % 8))
+
+        def turn_vectors():
+            near_bank = bank(6)
+            dealt_bank = bank(7)
+            for t in range(PACK):
+                nc.tensor.transpose(near_bank[:, t * P : (t + 1) * P], vec_rows[:, t * P : (t + 1) * P], ident[:])
+            for t in range(PACK):
+                nc.tensor.transpose(dealt_bank[:, t * P : (t + 1) * P], vec_rows[:, t:SPAN:PACK], ident[:])
+            near_view = near_bank[:].rearrange("p (t n) -> p t n", t=PACK)
+            nc.scalar.copy(near_cols[:], near_view[:, :, :VEC_ROWS])
+            nc.scalar.activation(neg_slot[:], near_view[:, :, 4:6], ACT.Copy, scale=-1.0)
+            nc.scalar.copy(dealt_cols[:], dealt_bank[:].rearrange("p (t n) -> p t n", t=PACK)[:, :, 2:4])
 
         sums = {}
 
@@ -295,11 +307,12 @@ def tile_list_parcel_boundary_conflicts_kernel(
 
         def make_x(i):
             b, t = divmod(i, PACK)
+            cols = near_cols if b == 0 else dealt_cols
             if b == 0:
                 dst = near[i][:, T2:]
             else:
                 dst = x_pair[t // 2][:, t % 2, :]
-            nc.vector.tensor_scalar(dst, picked[i][:], low_sb[b][:, t : t + 1], gain_sb[b][:, t : t + 1], ALU.max, ALU.mult)
+            nc.vector.tensor_scalar(dst, picked[i][:], cols[:, t, 0:1], cols[:, t, 1:2], ALU.max, ALU.mult)
             if b == 0:
                 move_rows(i)
                 load_late(i)
@@ -340,6 +353,7 @@ def tile_list_parcel_boundary_conflicts_kernel(
         round_w1_near(1)
         quantize_w1(1)
         first_products(1)
+        turn_vectors()
 
         for i in range(TILES - 1):
             put(i)
@@ -376,7 +390,6 @@ def tile_list_parcel_boundary_conflicts_kernel(
         for n in range(TILES):
             last_product(n, 0)
         last = TILES - 1
-        nc.scalar.activation(neg_slot[:], slot_sb[:], ACT.Copy, scale=-1.0)
         put(last)
         round_page(last)
         fetch(last)
@@ -396,7 +409,7 @@ def tile_list_parcel_boundary_conflicts_kernel(
         def shift(n):
             if n not in VECTOR_ONLY:
                 shifted[n] = ring.tile([P, NX], F32, name="shifted", bufs=4)
-                nc.scalar.activation(shifted[n][:], scores[n][:], ACT.Identity, bias=neg_slot[:, n : n + 1])
+                nc.scalar.activation(shifted[n][:], scores[n][:], ACT.Identity, bias=neg_slot[:, n % PACK, n // PACK : n // PACK + 1])
 
         def count_turns(n):
             if n == 0:
@@ -404,7 +417,7 @@ def tile_list_parcel_boundary_conflicts_kernel(
             else:
                 turns[n] = ring.tile([P, NX], I32, name="work_a")
             if n in VECTOR_ONLY:
-                nc.vector.tensor_scalar(turns[n][:], scores[n][:], slot_sb[:, n : n + 1], 1.0 / TWO_PI, ALU.subtract, ALU.mult)
+                nc.vector.tensor_scalar(turns[n][:], scores[n][:], near_cols[:, n % PACK, 4 + n // PACK : 5 + n // PACK], 1.0 / TWO_PI, ALU.subtract, ALU.mult)
             else:
                 nc.vector.tensor_scalar(turns[n][:], shifted[n][:], 1.0 / TWO_PI, None, ALU.mult)
 
@@ -417,7 +430,7 @@ def tile_list_parcel_boundary_conflicts_kernel(
                 result = held("result%d" % part if parts > 1 else "prior%d" % n, [P, wide], F32)
                 if n in VECTOR_ONLY:
                     nc.vector.scalar_tensor_tensor(reduced[:], turns[n][:, cols], -TWO_PI, scores[n][:, cols], ALU.mult, ALU.add)
-                    nc.scalar.activation(result[:], reduced[:], ACT.Sin, bias=neg_slot[:, n : n + 1])
+                    nc.scalar.activation(result[:], reduced[:], ACT.Sin, bias=neg_slot[:, n % PACK, n // PACK : n // PACK + 1])
                 else:
                     nc.vector.scalar_tensor_tensor(reduced[:], turns[n][:, cols], -TWO_PI, shifted[n][:, cols], ALU.mult, ALU.add)
                     nc.scalar.activation(result[:], reduced[:], ACT.Sin)

@@ -23,8 +23,8 @@ PACK = 4
 SPAN = P * PACK
 PASSES = 2
 TILES = PASSES * PACK
-CHUNK_EDGES = (0, 128, 256, 512, 1024)
-CHUNKS = len(CHUNK_EDGES) - 1
+CHUNK_EDGES = ((0, 1024), (0, 128, 256, 512, 1024))
+CHUNKS = len(CHUNK_EDGES[1]) - 1
 VEC_ROWS = 6
 TWO_PI = 2.0 * math.pi
 VECTOR_ONLY = (0, 4)
@@ -56,7 +56,7 @@ def tile_list_parcel_boundary_conflicts_kernel(
         prior_sb = [held("prior%d" % i, [P, S], F32) for i in range(TILES)]
         page = [held("page%d" % i, [P, T2], F32) for i in range(TILES)]
         wgs_near = held("wgs_near", [P, S], F32)
-        wgs_dealt = held("wgs_dealt", [P, PACK, S], F32)
+        wgs_dealt = [held("wgs_dealt%d" % u, [P, 2, S], F32) for u in range(2)]
         vec_rows = held("vec_rows", [P, SPAN], F32)
         ident = held("ident", [P, P], F32)
         near_cols = held("near_cols", [P, PACK, VEC_ROWS], F32)
@@ -129,9 +129,10 @@ def tile_list_parcel_boundary_conflicts_kernel(
         load_prior(4)
 
         def load_late(i):
-            if i == 0:
+            if i % 2 == 0:
+                rows = wgs.rearrange("(q t) j -> q t j", t=PACK)[:, i : i + 2, :]
                 for q in (0, 2, 1, 3):
-                    nc.sync.dma_start(wgs_dealt[32 * q : 32 * q + 32], wgs.rearrange("(q t) j -> q t j", t=PACK))
+                    nc.sync.dma_start(wgs_dealt[i // 2][32 * q : 32 * q + 32], rows)
             load_page(PACK + i)
             if PACK + i + 1 < TILES:
                 load_prior(PACK + i + 1)
@@ -239,7 +240,7 @@ def tile_list_parcel_boundary_conflicts_kernel(
             nc.vector.tensor_tensor(h[i][:], sums[i][1][:], raised[i][:], ALU.min)
 
         def put(i):
-            factors = wgs_near[:] if i < PACK else wgs_dealt[:, i - PACK, :]
+            factors = wgs_near[:] if i < PACK else wgs_dealt[(i - PACK) // 2][:, i % 2, :]
             nc.vector.tensor_tensor(page[i][:].indirect(idx2[:]), h[i][:], factors, ALU.mult)
 
         def fetch(i):
@@ -251,15 +252,16 @@ def tile_list_parcel_boundary_conflicts_kernel(
                 picked[i] = ring.tile([P, NX], F32, name="work_c")
             nc.vector.tensor_copy(picked[i][:], page[i][:].indirect(idx3[:]))
 
-        def width(c):
-            return CHUNK_EDGES[c + 1] - CHUNK_EDGES[c]
+        def width(b, c):
+            return CHUNK_EDGES[b][c + 1] - CHUNK_EDGES[b][c]
 
         def span(c):
-            return slice(CHUNK_EDGES[c], CHUNK_EDGES[c + 1])
+            return slice(CHUNK_EDGES[1][c], CHUNK_EDGES[1][c + 1])
 
-        page_b = {(b, c): held("page_b%d%d" % (b, c), [P, width(c), PACK], BF16) for b in range(PASSES) for c in range(CHUNKS)}
+        chunks = [(b, c) for b in range(PASSES) for c in range(len(CHUNK_EDGES[b]) - 1)]
+        page_b = {(b, c): held("page_b%d%d" % (b, c), [P, width(b, c), PACK], BF16) for b, c in chunks}
         page_c = {}
-        page_s = {(b, c): held("page_s%d%d" % (b, c), [P, width(c)], U8) for b in range(PASSES) for c in range(CHUNKS)}
+        page_s = {(b, c): held("page_s%d%d" % (b, c), [P, width(b, c)], U8) for b, c in chunks}
         x_b = [held("x_b0", [P, NX, PACK], BF16)]
         x_c = [held("x_c%d" % b, [P, NX], U32) for b in range(PASSES)]
         x_s = [held("x_s%d" % b, [P, NX], U8) for b in range(PASSES)]
@@ -271,7 +273,7 @@ def tile_list_parcel_boundary_conflicts_kernel(
 
         def round_page(i):
             if i < PACK:
-                near[i] = held(("w1_near1", "w1_near2", "w1_raw0", "w1_raw1")[i], [P, T2 + NX], BF16)
+                near[i] = held(("w1_near1", "w1_near2", "w1_near3", "w1_raw1")[i], [P, T2 + NX], BF16)
                 nc.scalar.copy(near[i][:, :T2], page[i][:])
             elif i < TILES - 1:
                 nc.scalar.copy(staged[0][:, i - PACK, :], page[i][:])
@@ -290,11 +292,10 @@ def tile_list_parcel_boundary_conflicts_kernel(
                 nc.sync.dma_start(gathered[32 * i : 32 * (i + 1), t, :], near[i][t:P:PACK, :])
 
         def weave():
-            for c in range(CHUNKS):
-                nc.scalar.copy(
-                    page_b[0, c][:].rearrange("p (m e) t -> p m t e", e=4),
-                    gathered[:, :, span(c)].rearrange("p t (m e) -> p m t e", e=4),
-                )
+            nc.scalar.copy(
+                page_b[0, 0][:].rearrange("p (m e) t -> p m t e", e=4),
+                gathered[:, :, :T2].rearrange("p t (m e) -> p m t e", e=4),
+            )
             nc.scalar.copy(
                 x_b[0][:].rearrange("p (m e) t -> p m t e", e=4),
                 gathered[:, :, T2:].rearrange("p t (m e) -> p m t e", e=4),
@@ -302,7 +303,7 @@ def tile_list_parcel_boundary_conflicts_kernel(
 
         def quantize_page(b, c):
             name = "x_pair1" if (b, c) == (1, CHUNKS - 1) else "page_c%d%d" % (b, c)
-            page_c[b, c] = held(name, [P, width(c)], U32)
+            page_c[b, c] = held(name, [P, width(b, c)], U32)
             nc.vector.quantize_mx(page_c[b, c][:].bitcast(FP8X4), page_s[b, c][:], page_b[b, c][:].rearrange("p m t -> p (m t)"))
 
         def make_x(i):
@@ -328,8 +329,9 @@ def tile_list_parcel_boundary_conflicts_kernel(
         scores = {}
 
         def last_product(n, b):
-            c = max(k for k in range(CHUNKS) if CHUNK_EDGES[k] <= n * P)
-            cols = slice(n * P - CHUNK_EDGES[c], (n + 1) * P - CHUNK_EDGES[c])
+            edges = CHUNK_EDGES[b]
+            c = max(k for k in range(len(edges) - 1) if edges[k] <= n * P)
+            cols = slice(n * P - edges[c], (n + 1) * P - edges[c])
             if b == 0:
                 scores[n] = bank(n)
             nc.tensor.matmul_mx(
@@ -367,8 +369,7 @@ def tile_list_parcel_boundary_conflicts_kernel(
             round_page(i)
             raise_to_prior(i + 1)
             if i == TILES - 2:
-                for c in range(CHUNKS):
-                    quantize_page(0, c)
+                quantize_page(0, 0)
                 quantize_x(0)
             fetch(i)
             cap(i + 1)

import math
from contextlib import ExitStack

import concourse.mybir as mybir
from concourse.masks import make_identity

T, S, K, H, T2, NX = 2048, 512, 1024, 1024, 1024, 512
FLOPS = 2 * (2 * K * H * S + H * T2 * NX)

F32 = mybir.dt.float32
BF16 = mybir.dt.bfloat16
I32 = mybir.dt.int32
U32 = mybir.dt.uint32
U16 = mybir.dt.uint16
U8 = mybir.dt.uint8
FP8X4 = mybir.dt.float8_e4m3fn_x4
FP4X4 = mybir.dt.float4_e2m1fn_x4
ALU = mybir.AluOpType
ACT = mybir.ActivationFunctionType

P = 128
PACK = 4
SPAN = P * PACK
PASSES = 2
TILES = PASSES * PACK
CHUNK_EDGES = ((0, 1024), (0, 128, 256, 512, 1024))
CHUNKS = len(CHUNK_EDGES[1]) - 1
VEC_ROWS = 6
TWO_PI = 2.0 * math.pi
VECTOR_ONLY = (0, 4)


def tile_list_parcel_boundary_conflicts_kernel(
    tc, tab_words, tab_scales, offs, w1, w4_words, w4_scales, prior, wgs, page0, offs2, offs3, low, gain, slot, out
):
    nc = tc.nc
    with ExitStack() as ctx:
        lists = ctx.enter_context(tc.tile_pool(name="lists", bufs=1))
        keep = ctx.enter_context(tc.tile_pool(name="keep", bufs=1))
        ring = ctx.enter_context(tc.tile_pool(name="ring", bufs=3))
        psum = ctx.enter_context(tc.psum_pool(name="psum", bufs=1))

        def held(name, shape, dtype):
            return keep.tile(shape, dtype, name=name, align_bytes=64)

        idx = lists.tile([P, S // 16], U16, name="idx")
        idx2 = lists.tile([P, S // 16], U16, name="idx2")
        idx3 = lists.tile([P, NX // 16], U16, name="idx3")

        tab_w = [held("tab_w%d" % a, [P, T], U32) for a in range(PASSES)]
        tab_s = held("tab_s", [P, PASSES * T], U8)
        w4_raw = held("w4_raw", [P, PASSES, 2 * H], U8)
        w4s_raw = held("w4s_raw", [P, PASSES * H], U8)
        w1_near = [held("w1_near%d" % i, [P, PASSES, PACK, P], F32) for i in range(PACK)]
        w1_raw = [held("w1_raw%d" % a, [P, PACK, SPAN], F32) for a in range(PASSES)]
        prior_sb = [held("prior%d" % i, [P, S], F32) for i in range(TILES)]
        page = [held("page%d" % i, [P, T2], F32) for i in range(TILES)]
        wgs_near = held("wgs_near", [P, S], F32)
        wgs_dealt = [held("wgs_dealt%d" % u, [P, 2, S], F32) for u in range(2)]
        vec_rows = held("vec_rows", [P, SPAN], F32)
        ident = held("ident", [P, P], F32)
        near_cols = held("near_cols", [P, PACK, VEC_ROWS], F32)
        dealt_cols = held("dealt_cols", [P, PACK, 2], F32)
        neg_slot = held("neg_slot", [P, PACK, 2], F32)
        warm_in = held("warm_in", [P, 1], F32)
        warm_out = held("warm_out", [P, 1], F32)

        nc.vector.memset(tab_s[:].bitcast(I32), 0)
        nc.vector.memset(w4s_raw[:].bitcast(I32), 0)
        nc.vector.memset(warm_in[:], 0.0)
        nc.gpsimd.memset(vec_rows[:], 0.0)
        make_identity(nc, ident[:])
        nc.scalar.activation(warm_out[:], warm_in[:], ACT.Sin)

        def load_tab(a):
            nc.sync.dma_start(tab_w[a][:].bitcast(I32), tab_words[a].rearrange("p t i -> p (t i)").bitcast(I32))

        def load_planes(dst, src):
            rows = src.bitcast(I32).rearrange("a (q r) n -> r q a n", r=4)
            for r in range(4):
                nc.sync.dma_start(dst[r:P:32, :].bitcast(I32).rearrange("p (a n) -> p a n", a=PASSES), rows[r])

        def load_w1_near(i):
            for a in range(PASSES):
                rows = w1[a * SPAN : (a + 1) * SPAN, i * P : (i + 1) * P]
                nc.sync.dma_start(w1_near[i][:, a], rows.rearrange("(p j) c -> p j c", j=PACK))

        def load_w1(a):
            rows = w1[a * SPAN : (a + 1) * SPAN, SPAN : 2 * SPAN]
            nc.sync.dma_start(w1_raw[a][:], rows.rearrange("(p j) c -> p j c", j=PACK))

        def rows_of(src, i):
            if i < PACK:
                return src[i * P : (i + 1) * P, :]
            return src[SPAN:, :].rearrange("(p t) n -> t p n", t=PACK)[i - PACK]

        def load_prior(i):
            nc.sync.dma_start(prior_sb[i][:], rows_of(prior, i))

        def load_page(i):
            nc.sync.dma_start(page[i][:], rows_of(page0, i))

        nc.sync.dma_start(idx[:], offs)
        load_tab(0)
        load_w1_near(0)
        load_planes(tab_s, tab_scales)
        load_tab(1)
        nc.sync.dma_start(w4_raw[:].bitcast(I32), w4_words.bitcast(I32).rearrange("a p n -> p a n"))
        load_planes(w4s_raw, w4_scales)
        load_prior(0)
        nc.sync.dma_start(wgs_near[:], wgs)
        load_page(0)
        nc.sync.dma_start(idx2[:], offs2)
        load_w1_near(1)
        load_prior(1)
        nc.sync.dma_start(idx3[:], offs3)
        nc.sync.dma_start(vec_rows[0:3:2, :], low.rearrange("(b n) -> b n", b=PASSES))
        nc.sync.dma_start(vec_rows[1:4:2, :], gain.rearrange("(b n) -> b n", b=PASSES))
        nc.sync.dma_start(vec_rows[4:6, :], slot.rearrange("(b n) -> b n", b=2))
        load_w1_near(2)
        load_page(1)
        load_prior(2)
        load_w1_near(3)
        load_page(2)
        load_prior(3)
        load_w1(0)
        load_w1(1)
        load_page(3)
        load_prior(4)

        def load_late(i):
            if i % 2 == 0:
                rows = wgs.rearrange("(q t) j -> q t j", t=PACK)[:, i : i + 2, :]
                for q in (0, 2, 1, 3):
                    nc.sync.dma_start(wgs_dealt[i // 2][32 * q : 32 * q + 32], rows)
            load_page(PACK + i)
            if PACK + i + 1 < TILES:
                load_prior(PACK + i + 1)

        v_w = [held("v_w%d" % a, [P, S], U32) for a in range(PASSES)]
        v_s = [held("v_s%d" % a, [P, S], U8) for a in range(PASSES)]

        def pick_words(a):
            nc.vector.tensor_copy(v_w[a][:], tab_w[a][:].indirect(idx[:]))

        def pick_scales(a):
            nc.vector.tensor_copy(v_s[a][:], tab_s[:, a * T : (a + 1) * T].indirect(idx[:]))

        w4_c = [held("w4_c%d" % a, [P, PACK, 2 * P], U8) for a in range(PASSES)]
        w4_s = [held("w4_s%d" % a, [P, PACK, P], U8) for a in range(PASSES)]
        w1_b = {}
        w1_c = {}
        w1_s = {}

        def deal_w4(a):
            src = w4_raw[:, a, 2 * SPAN :].bitcast(U16).rearrange("p (q t) -> p t q", t=PACK)
            nc.vector.tensor_copy(w4_c[a][:].bitcast(U16), src)

        def deal_w4_scales(a):
            src = w4s_raw[:, a * H + SPAN : (a + 1) * H].rearrange("p (q t) -> p t q", t=PACK)
            nc.vector.tensor_copy(w4_s[a][:], src)

        def round_w1_near(i):
            w1_b[i] = ring.tile([P, 2, P, PACK], BF16, name="w1_b", align_bytes=64, bufs=6)
            for a in range(PASSES):
                nc.scalar.copy(
                    w1_b[i][:, a].rearrange("p (c e) j -> p c j e", e=4),
                    w1_near[i][:, a].rearrange("p j (c e) -> p c j e", e=4),
                )

        def round_w1(a, u):
            w1_b[a, u] = ring.tile([P, 2, P, PACK], BF16, name="w1_b", align_bytes=64, bufs=6)
            nc.scalar.copy(
                w1_b[a, u][:].rearrange("p t q j -> p q j t"),
                w1_raw[a][:].rearrange("p j (q t) -> p q j t", t=PACK)[:, :, :, 2 * u : 2 * u + 2],
            )

        def quantize_w1(key):
            name = "%d" % key if isinstance(key, int) else "%d%d" % key
            w1_c[key] = held("w1_c" + name, [P, 2 * P], U32)
            w1_s[key] = held("w1_s" + name, [P, 2 * P], U8)
            nc.vector.quantize_mx(w1_c[key][:].bitcast(FP8X4), w1_s[key][:], w1_b[key][:].rearrange("p t q j -> p (t q j)"))

        def bank(n):
            return psum.tile([P, 512], F32, name="bank%d" % (n % 8))

        def turn_vectors():
            near_bank = bank(6)
            dealt_bank = bank(7)
            for t in range(PACK):
                nc.tensor.transpose(near_bank[:, t * P : (t + 1) * P], vec_rows[:, t * P : (t + 1) * P], ident[:])
            for t in range(PACK):
                nc.tensor.transpose(dealt_bank[:, t * P : (t + 1) * P], vec_rows[:, t:SPAN:PACK], ident[:])
            near_view = near_bank[:].rearrange("p (t n) -> p t n", t=PACK)
            nc.scalar.copy(near_cols[:], near_view[:, :, :VEC_ROWS])
            nc.scalar.activation(neg_slot[:], near_view[:, :, 4:6], ACT.Copy, scale=-1.0)
            nc.scalar.copy(dealt_cols[:], dealt_bank[:].rearrange("p (t n) -> p t n", t=PACK)[:, :, 2:4])

        sums = {}

        def first_products(i):
            first = bank(2 * i)
            second = bank(2 * i + 1)
            for a in range(PASSES):
                if i < PACK:
                    key, e = i, a
                else:
                    key, e = (a, (i - PACK) // 2), i % 2
                cols = slice(e * P, (e + 1) * P)
                nc.tensor.matmul_mx(
                    first[:], w1_c[key][:, cols].bitcast(FP8X4), w1_s[key][:, cols],
                    v_w[a][:].bitcast(FP8X4), v_s[a][:], start=(a == 0), stop=(a == PASSES - 1),
                )
            for a in range(PASSES):
                if i < PACK:
                    codes = w4_raw[:, a, 2 * P * i : 2 * P * (i + 1)]
                    scales = w4s_raw[:, a * H + P * i : a * H + P * (i + 1)]
                else:
                    codes = w4_c[a][:, i - PACK, :]
                    scales = w4_s[a][:, i - PACK, :]
                nc.tensor.matmul_mx(
                    second[:], codes.bitcast(FP4X4), scales,
                    v_w[a][:].bitcast(FP8X4), v_s[a][:], start=(a == 0), stop=(a == PASSES - 1),
                )
            sums[i] = (first, second)

        raised = {}
        h = {}
        picked = {}

        def raise_to_prior(i):
            raised[i] = ring.tile([P, S], F32, name="work_a")
            nc.vector.tensor_tensor(raised[i][:], sums[i][0][:], prior_sb[i][:], ALU.max)

        def cap(i):
            if i == TILES - 1:
                h[i] = held("page%d" % (i - 1), [P, S], F32)
            else:
                h[i] = ring.tile([P, S], F32, name="work_b")
            nc.vector.tensor_tensor(h[i][:], sums[i][1][:], raised[i][:], ALU.min)

        def put(i):
            factors = wgs_near[:] if i < PACK else wgs_dealt[(i - PACK) // 2][:, i % 2, :]
            nc.vector.tensor_tensor(page[i][:].indirect(idx2[:]), h[i][:], factors, ALU.mult)

        def fetch(i):
            if i == TILES - 1:
                picked[i] = held("gathered", [P, NX], F32)
            elif i == TILES - 2:
                picked[i] = held("x_b0", [P, NX], F32)
            else:
                picked[i] = ring.tile([P, NX], F32, name="work_c")
            nc.vector.tensor_copy(picked[i][:], page[i][:].indirect(idx3[:]))

        def width(b, c):
            return CHUNK_EDGES[b][c + 1] - CHUNK_EDGES[b][c]

        def span(c):
            return slice(CHUNK_EDGES[1][c], CHUNK_EDGES[1][c + 1])

        chunks = [(b, c) for b in range(PASSES) for c in range(len(CHUNK_EDGES[b]) - 1)]
        page_b = {(b, c): held("page_b%d%d" % (b, c), [P, width(b, c), PACK], BF16) for b, c in chunks}
        page_c = {}
        page_s = {(b, c): held("page_s%d%d" % (b, c), [P, width(b, c)], U8) for b, c in chunks}
        x_b = [held("x_b0", [P, NX, PACK], BF16)]
        x_c = [held("x_c%d" % b, [P, NX], U32) for b in range(PASSES)]
        x_s = [held("x_s%d" % b, [P, NX], U8) for b in range(PASSES)]
        x_pair = [held("x_pair%d" % u, [P, 2, NX], BF16) for u in range(2)]
        gathered = held("gathered", [P, PACK, T2 + NX], BF16)
        near = {}

        staged = []

        def round_page(i):
            if i < PACK:
                near[i] = held(("w1_near1", "w1_near2", "w1_near3", "w1_raw1")[i], [P, T2 + NX], BF16)
                nc.scalar.copy(near[i][:, :T2], page[i][:])
            elif i < TILES - 1:
                nc.scalar.copy(staged[0][:, i - PACK, :], page[i][:])
                if i == TILES - 2:
                    for c in range(CHUNKS):
                        nc.scalar.copy(
                            page_b[1, c][:, :, : PACK - 1],
                            staged[0][:, :, span(c)].rearrange("p t m -> p m t"),
                        )
            else:
                for c in range(CHUNKS):
                    nc.scalar.copy(page_b[1, c][:, :, PACK - 1], page[i][:, span(c)])

        def move_rows(i):
            for t in range(PACK):
                nc.sync.dma_start(gathered[32 * i : 32 * (i + 1), t, :], near[i][t:P:PACK, :])

        def weave():
            nc.scalar.copy(
                page_b[0, 0][:].rearrange("p (m e) t -> p m t e", e=4),
                gathered[:, :, :T2].rearrange("p t (m e) -> p m t e", e=4),
            )
            nc.scalar.copy(
                x_b[0][:].rearrange("p (m e) t -> p m t e", e=4),
                gathered[:, :, T2:].rearrange("p t (m e) -> p m t e", e=4),
            )

        def quantize_page(b, c):
            name = "x_pair1" if (b, c) == (1, CHUNKS - 1) else "page_c%d%d" % (b, c)
            page_c[b, c] = held(name, [P, width(b, c)], U32)
            nc.vector.quantize_mx(page_c[b, c][:].bitcast(FP8X4), page_s[b, c][:], page_b[b, c][:].rearrange("p m t -> p (m t)"))

        def make_x(i):
            b, t = divmod(i, PACK)
            cols = near_cols if b == 0 else dealt_cols
            if b == 0:
                dst = near[i][:, T2:]
            else:
                dst = x_pair[t // 2][:, t % 2, :]
            nc.vector.tensor_scalar(dst, picked[i][:], cols[:, t, 0:1], cols[:, t, 1:2], ALU.max, ALU.mult)
            if b == 0:
                move_rows(i)
                load_late(i)
            elif t == 1:
                nc.scalar.copy(x_b[b][:, :, 0:2], x_pair[0][:].rearrange("p e j -> p j e"))

        def weave_last_pair():
            nc.vector.tensor_copy(x_b[1][:, :, 2:4], x_pair[1][:].rearrange("p e j -> p j e"))

        def quantize_x(b):
            nc.vector.quantize_mx(x_c[b][:].bitcast(FP8X4), x_s[b][:], x_b[b][:].rearrange("p j t -> p (j t)"))

        scores = {}

        def last_product(n, b):
            edges = CHUNK_EDGES[b]
            c = max(k for k in range(len(edges) - 1) if edges[k] <= n * P)
            cols = slice(n * P - edges[c], (n + 1) * P - edges[c])
            if b == 0:
                scores[n] = bank(n)
            nc.tensor.matmul_mx(
                scores[n][:], page_c[b, c][:, cols].bitcast(FP8X4), page_s[b, c][:, cols],
                x_c[b][:].bitcast(FP8X4), x_s[b][:], start=(b == 0), stop=(b == PASSES - 1),
            )

        pick_words(0)
        round_w1_near(0)
        pick_scales(0)
        quantize_w1(0)
        pick_scales(1)
        pick_words(1)
        first_products(0)
        for a in range(PASSES):
            deal_w4(a)
        raise_to_prior(0)
        deal_w4_scales(0)
        cap(0)
        deal_w4_scales(1)
        round_w1_near(1)
        quantize_w1(1)
        first_products(1)
        turn_vectors()

        for i in range(TILES - 1):
            put(i)
            if i + 2 < PACK:
                round_w1_near(i + 2)
            if i == 1:
                round_w1(0, 0)
                round_w1(1, 0)
                round_w1(0, 1)
                round_w1(1, 1)
            round_page(i)
            raise_to_prior(i + 1)
            if i == TILES - 2:
                quantize_page(0, 0)
                quantize_x(0)
            fetch(i)
            cap(i + 1)
            make_x(i)
            if i + 2 < PACK:
                quantize_w1(i + 2)
            if i == 2:
                quantize_w1((0, 0))
                quantize_w1((1, 0))
            if i == 3:
                quantize_w1((0, 1))
                quantize_w1((1, 1))
            if i + 2 < TILES:
                first_products(i + 2)
            if i == 3:
                weave()
                staged.append(held("gathered", [P, PACK - 1, T2], BF16))
                x_b.append(held("w1_raw1", [P, NX, PACK], BF16))
        for n in range(TILES):
            last_product(n, 0)
        last = TILES - 1
        put(last)
        round_page(last)
        fetch(last)
        quantize_page(1, 0)
        make_x(last)
        quantize_page(1, 1)
        weave_last_pair()
        quantize_page(1, 2)
        quantize_x(1)
        quantize_page(1, 3)
        for n in range(TILES):
            last_product(n, 1)

        shifted = {}
        turns = {}

        def shift(n):
            if n not in VECTOR_ONLY:
                shifted[n] = ring.tile([P, NX], F32, name="shifted", bufs=4)
                nc.scalar.activation(shifted[n][:], scores[n][:], ACT.Identity, bias=neg_slot[:, n % PACK, n // PACK : n // PACK + 1])

        def count_turns(n):
            if n == 0:
                turns[n] = held("page_b1%d" % (CHUNKS - 1), [P, NX], I32)
            else:
                turns[n] = ring.tile([P, NX], I32, name="work_a")
            if n in VECTOR_ONLY:
                nc.vector.tensor_scalar(turns[n][:], scores[n][:], near_cols[:, n % PACK, 4 + n // PACK : 5 + n // PACK], 1.0 / TWO_PI, ALU.subtract, ALU.mult)
            else:
                nc.vector.tensor_scalar(turns[n][:], shifted[n][:], 1.0 / TWO_PI, None, ALU.mult)

        def finish(n):
            parts = 2 if n == TILES - 1 else 1
            wide = NX // parts
            for part in range(parts):
                cols = slice(part * wide, (part + 1) * wide)
                reduced = ring.tile([P, wide], F32, name="work_b")
                result = held("result%d" % part if parts > 1 else "prior%d" % n, [P, wide], F32)
                if n in VECTOR_ONLY:
                    nc.vector.scalar_tensor_tensor(reduced[:], turns[n][:, cols], -TWO_PI, scores[n][:, cols], ALU.mult, ALU.add)
                    nc.scalar.activation(result[:], reduced[:], ACT.Sin, bias=neg_slot[:, n % PACK, n // PACK : n // PACK + 1])
                else:
                    nc.vector.scalar_tensor_tensor(reduced[:], turns[n][:, cols], -TWO_PI, shifted[n][:, cols], ALU.mult, ALU.add)
                    nc.scalar.activation(result[:], reduced[:], ACT.Sin)
                nc.sync.dma_start(out[n * P : (n + 1) * P, cols], result[:])

        shift(1)
        shift(2)
        count_turns(0)
        for n in range(TILES):
            if n + 3 < TILES:
                shift(n + 3)
            if n + 1 < TILES:
                count_turns(n + 1)
            finish(n)
